import numpy as np
import ml_dtypes


def mxq(x, axis, fmt="e4m3"):
    dtype, down = {"e4m3": (ml_dtypes.float8_e4m3fn, 7), "e5m2": (ml_dtypes.float8_e5m2, 14)}[fmt]
    v = np.moveaxis(np.asarray(x, np.float32).astype(ml_dtypes.bfloat16).astype(np.float64), axis, -1)
    blocks = v.reshape(v.shape[:-1] + (-1, 32))
    amax = np.abs(blocks).max(-1, keepdims=True)
    byte = np.maximum(np.where(amax > 0, np.frexp(amax)[1] - 1 + 127, 0) - down, 1)
    scale = np.exp2(byte - 127.0)
    codes = (blocks / scale).astype(np.float32).astype(dtype).astype(np.float64)
    return np.moveaxis((codes * scale).reshape(v.shape), -1, axis)


WIDE = False


def mx_kscale(k):
    if not WIDE:
        return np.ones(k)
    levels = np.array([10, -10, 5, -5, 0])
    if k % 512:
        return np.exp2(np.random.permutation(np.resize(levels, k // 32))).repeat(32)
    a = np.empty((k // 512, 16))
    for p in range(k // 512):
        a[p, :8] = np.random.permutation(np.resize(levels, 8))
        for g in range(8):
            far = levels[np.abs(levels - a[p, g]) >= 10]
            a[p, g + 8] = far[np.random.randint(len(far))]
    return np.exp2(a.ravel()).repeat(32)


def f64(x):
    return np.asarray(x).astype(np.float64)


def striped(idx):
    return np.tile(idx.reshape(-1, 16).T, (8, 1)).astype(np.uint16)


def unstriped(offs):
    return offs[:16].T.reshape(-1).astype(np.int64)


E2M1 = np.array([0.0, 0.5, 1.0, 1.5, 2.0, 3.0, 4.0, 6.0, -0.0, -0.5, -1.0, -1.5, -2.0, -3.0, -4.0, -6.0])


def pack_weight(w, fmt):
    k, n = w.shape
    w = f64(np.asarray(w, np.float32).astype(ml_dtypes.bfloat16)).reshape(k // 32, 32, n)
    amax = np.abs(w).max(1)
    if fmt == "e4m3":
        byte = np.frexp(amax)[1] - 1 + 127 - 7
    else:
        mant, ex = np.frexp(amax / 6.0)
        byte = np.where(mant > 0.5, ex, ex - 1) + 127
    byte = np.clip(np.where(amax > 0, byte, 1), 1, 254)
    scaled = (w * np.exp2(127.0 - byte)[:, None, :]).reshape(k, n).astype(np.float32)
    by_word = np.ascontiguousarray(scaled.reshape(k // 512, 128, 4, n).transpose(0, 1, 3, 2))
    if fmt == "e4m3":
        words = by_word.astype(ml_dtypes.float8_e4m3fn).view(np.uint8)
    else:
        c = by_word.astype(ml_dtypes.float4_e2m1fn).view(np.uint8) & 0xF
        words = (c[..., 0::2] | (c[..., 1::2] << 4)).reshape(k // 512, 128, 2 * n)
    return np.ascontiguousarray(words), np.ascontiguousarray(byte.astype(np.uint8).reshape(k // 512, 16, n))


def unpack_weight(words, scales, fmt):
    g, _, n = scales.shape
    words = np.ascontiguousarray(words).reshape(g, 128, n, -1)
    if fmt == "e4m3":
        vals = words.view(ml_dtypes.float8_e4m3fn).astype(np.float64)
    else:
        nib = np.empty((g, 128, n, 4), np.uint8)
        nib[..., 0::2] = words & 0xF
        nib[..., 1::2] = words >> 4
        vals = E2M1[nib]
    vals = vals * np.repeat(np.exp2(scales.astype(np.float64) - 127.0), 8, axis=1)[..., None]
    return vals.transpose(0, 1, 3, 2).reshape(g * 512, n)


def gelu(v):
    return 0.5 * v * (1.0 + np.tanh(np.sqrt(2.0 / np.pi) * (v + 0.044715 * v**3)))


K, T, E, C, N = 512, 2048, 8, 128, 256


def by_expert(wq, xq):
    return np.concatenate([wq[e].T @ xq[:, e * C:(e + 1) * C] for e in range(E)], axis=1)


def setup_inputs():
    n = np.random.standard_normal
    s = mx_kscale(K)[:, None]
    x = pack_weight(n((K, T)) * s, "e4m3")
    return {
        "x_words": x[0],
        "x_scales": x[1],
        "w": (n((E + 1, K, N)) / np.sqrt(K) / s[None]).astype(np.float32),
        "b": (0.3 * n((N, E + 1))).astype(np.float32),
        "gate": np.tile(np.random.uniform(0.2, 1.0, E * C), (N, 1)).astype(np.float32),
        "offs": striped(np.random.permutation(T)[:E * C]),
    }


def reference(x_words, x_scales, w, b, gate, offs):
    idx = unstriped(offs)
    wq = mxq(f64(w), 1, "e4m3")
    xs = unpack_weight(x_words, x_scales, "e4m3")
    ys = gelu((wq[E].T @ xs) + f64(b)[:, E:])
    xq = unpack_weight(x_words, x_scales, "e4m3")[:, idx]
    y = by_expert(wq, xq)
    y = gelu(y + np.repeat(f64(b)[:, :E], C, axis=1))
    out = ys
    out[:, idx] += f64(gate) * y
    return out

@@ -1,0 +1,163 @@
+from contextlib import ExitStack
+
+import concourse.mybir as mybir
+
+K, T, E, C, N = 512, 2048, 8, 128, 256
+SLOTS = E * C
+FLOPS = 2 * K * N * (T + SLOTS)
+BYTES = K * T + 16 * T + (E + 1) * K * N * 4 + N * (E + 1) * 4 + SLOTS * 4 + 128 * (SLOTS // 16) * 2 + N * T * 4
+
+F32 = mybir.dt.float32
+BF16 = mybir.dt.bfloat16
+I32 = mybir.dt.int32
+U32 = mybir.dt.uint32
+U16 = mybir.dt.uint16
+U8 = mybir.dt.uint8
+FP8X4 = mybir.dt.float8_e4m3fn_x4
+GELU = mybir.ActivationFunctionType.Gelu_apprx_tanh
+MULT = mybir.AluOpType.mult
+ADD = mybir.AluOpType.add
+
+P = 128
+PACK = 4
+HALVES = N // P
+PAIR = 2 * C
+PAIRS = E // 2
+CHUNK = 512
+CHUNKS = T // CHUNK
+
+
+def tile_moe_shr_lin_gelu_kernel(tc, x_words, x_scales, w, b, gate, offs, out):
+    nc = tc.nc
+    with ExitStack() as ctx:
+        lists = ctx.enter_context(tc.tile_pool(name="lists", bufs=1))
+        keep = ctx.enter_context(tc.tile_pool(name="keep", bufs=1))
+        routed_ps = ctx.enter_context(tc.psum_pool(name="routed_ps", bufs=4))
+        shared_ps = ctx.enter_context(tc.psum_pool(name="shared_ps", bufs=2))
+
+        offsets = lists.tile([P, SLOTS // 16], U16, name="offsets")
+        nc.sync.dma_start(offsets[:], offs)
+
+        W = PACK * N
+        first = [keep.tile([P, W], F32, name=f"first{e}") for e in range(2)]
+        later = keep.tile([P, (E + 1) * W], F32, name="later")
+        raw = [t[:] for t in first] + [later[:, (e - 2) * W:(e - 1) * W] for e in range(2, E + 1)]
+        gates = later[:, (E - 1) * W:E * W]
+        bias = later[:, E * W:E * W + HALVES * (E + 1)].rearrange("p (h e) -> p h e", h=HALVES)
+
+        def load_w(e, queue):
+            queue.dma_start(raw[e], w[e].rearrange("(p j) n -> p (j n)", j=PACK))
+
+        load_w(0, nc.scalar)
+        load_w(1, nc.scalar)
+
+        warm = keep.tile([P, (E + 1) * PACK], F32, name="warm", tag="token_words", align_bytes=64)
+        nc.vector.memset(warm[:], 0.0)
+        nc.scalar.activation(later[:, 0:(E + 1) * W:PAIR], warm[:], GELU)
+
+        token_scales = keep.tile([P, T], U8, name="token_scales", align_bytes=64)
+        nc.vector.memset(token_scales[:].bitcast(I32), 0)
+        for r in range(4):
+            nc.sync.dma_start(token_scales[r:P:32, :].bitcast(I32), x_scales[0, r:16:4, :].bitcast(I32))
+
+        windows = [keep.tile([P, T], F32, name=f"window{h}") for h in range(HALVES)]
+        for h in range(HALVES):
+            nc.vector.memset(windows[h][:], 0.0)
+
+        token_words = keep.tile([P, T], I32, name="token_words", tag="token_words", align_bytes=64)
+        nc.sync.dma_start(token_words[:], x_words[0].rearrange("p t r -> p (t r)").bitcast(I32))
+        nc.sync.dma_start(bias, b.rearrange("(h p) e -> p h e", p=P))
+        load_w(2, nc.sync)
+        nc.sync.dma_start(gates[:, 0:PAIR], gate[0:P, 0:PAIR])
+        load_w(3, nc.sync)
+        nc.sync.dma_start(gates[:, PAIR:SLOTS], gate[0:P, PAIR:SLOTS])
+        for e in (E, 4, 5, 6, 7):
+            load_w(e, nc.sync)
+
+        weights = {}
+
+        def quantize(*experts):
+            n = len(experts)
+            e0 = experts[0]
+            grouped = keep.tile([P, n * W], BF16, name=f"grouped{e0}", align_bytes=64)
+            for i, e in enumerate(experts):
+                nc.scalar.copy(
+                    grouped[:, i * W:(i + 1) * W].rearrange("p (c i j) -> p c j i", i=4, j=PACK),
+                    raw[e].rearrange("p (j c i) -> p c j i", i=4, j=PACK),
+                )
+            codes = keep.tile([P, n * N], U32, name=f"codes{e0}", align_bytes=64)
+            scales = keep.tile([P, n * N], U8, name=f"scales{e0}", align_bytes=64)
+            nc.vector.quantize_mx(out=codes[:].bitcast(FP8X4), scales=scales[:], in_=grouped[:])
+            for i, e in enumerate(experts):
+                weights[e] = codes[:, i * N:(i + 1) * N], scales[:, i * N:(i + 1) * N]
+
+        slot_words = []
+
+        def gather_words(g, tag):
+            sw = keep.tile([P, PAIR], U32, name=f"slot_words{g}", tag=tag, align_bytes=64)
+            nc.vector.tensor_copy(sw[:], token_words[:].bitcast(U32).indirect(offsets[:, g * PAIR // 16:(g + 1) * PAIR // 16]))
+            slot_words.append(sw)
+
+        slot_scales = keep.tile([P, SLOTS], U8, name="slot_scales", align_bytes=64)
+        nc.vector.tensor_copy(slot_scales[:], token_scales[:].indirect(offsets[:]))
+        quantize(0, 1)
+        for g in range(PAIRS):
+            gather_words(g, f"slot_words{g}")
+
+        def routed(g, h, y):
+            acc = routed_ps.tile([P, PAIR], F32, name="acc_routed")
+            cols = slice(h * P, (h + 1) * P)
+            for i in range(2):
+                codes, scales = weights[2 * g + i]
+                nc.tensor.matmul_mx(
+                    out=acc[:, i * C:(i + 1) * C],
+                    lhsT=codes[:, cols].bitcast(FP8X4), lhsT_scale=scales[:, cols],
+                    rhs=slot_words[g][:, i * C:(i + 1) * C].bitcast(FP8X4),
+                    rhs_scale=slot_scales[:, g * PAIR + i * C:g * PAIR + (i + 1) * C],
+                    start=True, stop=True,
+                )
+            for i in range(2):
+                e = 2 * g + i
+                nc.scalar.activation(y[:, i * C:(i + 1) * C], acc[:, i * C:(i + 1) * C], GELU, bias=bias[:, h, e:e + 1])
+            nc.vector.tensor_tensor(windows[h][:].indirect(offsets[:, g * PAIR // 16:(g + 1) * PAIR // 16]), y, gates[:, g * PAIR:(g + 1) * PAIR], MULT)
+
+        def shared(h, c, ys):
+            codes, scales = weights[E]
+            acc = shared_ps.tile([P, CHUNK], F32, name="acc_shared")
+            cols = slice(h * P, (h + 1) * P)
+            toks = slice(c * CHUNK, (c + 1) * CHUNK)
+            nc.tensor.matmul_mx(
+                out=acc[:], lhsT=codes[:, cols].bitcast(FP8X4), lhsT_scale=scales[:, cols],
+                rhs=token_words[:, toks].bitcast(FP8X4), rhs_scale=token_scales[:, toks],
+                start=True, stop=True,
+            )
+            nc.scalar.activation(ys, acc[:], GELU, bias=bias[:, h, E:E + 1])
+
+        def finish(h, t0, t1, ys):
+            total = keep.tile([P, t1 - t0], F32, name=f"total{h}_{t0}")
+            nc.vector.tensor_tensor(total[:], windows[h][:, t0:t1], ys, ADD)
+            nc.sync.dma_start(out[h * P:(h + 1) * P, t0:t1], total[:])
+
+        for g in range(PAIRS - 1):
+            y0 = keep.tile([P, PAIR], F32, name=f"y{g}")
+            routed(g, 0, y0[:])
+            quantize(2 * g + 2, 2 * g + 3)
+            routed(g, 1, raw[2 * g + 3][:, 0:PAIR])
+            if g == 0:
+                quantize(E)
+        y_last = keep.tile([P, PAIR], F32, name="y_last")
+        routed(PAIRS - 1, 0, y_last[:])
+
+        ys_own = [keep.tile([P, CHUNK], F32, name=f"ys{i}") for i in range(CHUNKS - 2)]
+        ys_first = [raw[E - 2][:, 0:CHUNK], raw[E - 2][:, CHUNK:2 * CHUNK]] + [t[:] for t in ys_own]
+        ys_second = keep.tile([P, T], F32, name="ys_second")
+        for c in range(CHUNKS):
+            shared(0, c, ys_first[c])
+        for c in range(CHUNKS):
+            finish(0, c * CHUNK, (c + 1) * CHUNK, ys_first[c])
+        for c in range(CHUNKS):
+            shared(1, c, ys_second[:, c * CHUNK:(c + 1) * CHUNK])
+        routed(PAIRS - 1, 1, ys_first[2][:, 0:PAIR])
+        cuts = [0, 256, 768, 1280, 1792, T]
+        for t0, t1 in zip(cuts, cuts[1:]):
+            finish(1, t0, t1, ys_second[:, t0:t1])

@@ -39,7 +39,7 @@ def tile_moe_shr_lin_gelu_kernel(tc, x_words, x_scales, w, b, gate, offs, out):
         nc.sync.dma_start(offsets[:], offs)
 
         W = PACK * N
-        first = [keep.tile([P, W], F32, name=f"first{e}") for e in range(2)]
+        first = [keep.tile([P, W], F32, name=f"first{e}", tag=f"first{e}") for e in range(2)]
         later = keep.tile([P, (E + 1) * W], F32, name="later")
         raw = [t[:] for t in first] + [later[:, (e - 2) * W:(e - 1) * W] for e in range(2, E + 1)]
         gates = later[:, (E - 1) * W:E * W]
@@ -51,28 +51,26 @@ def tile_moe_shr_lin_gelu_kernel(tc, x_words, x_scales, w, b, gate, offs, out):
         load_w(0, nc.scalar)
         load_w(1, nc.scalar)
 
-        warm = keep.tile([P, (E + 1) * PACK], F32, name="warm", tag="token_words", align_bytes=64)
-        nc.vector.memset(warm[:], 0.0)
-        nc.scalar.activation(later[:, 0:(E + 1) * W:PAIR], warm[:], GELU)
-
         token_scales = keep.tile([P, T], U8, name="token_scales", align_bytes=64)
         nc.vector.memset(token_scales[:].bitcast(I32), 0)
         for r in range(4):
             nc.sync.dma_start(token_scales[r:P:32, :].bitcast(I32), x_scales[0, r:16:4, :].bitcast(I32))
 
-        windows = [keep.tile([P, T], F32, name=f"window{h}") for h in range(HALVES)]
-        for h in range(HALVES):
-            nc.vector.memset(windows[h][:], 0.0)
+        warm = keep.tile([P, (E + 1) * PACK], F32, name="warm", tag="token_words", align_bytes=64)
+        nc.vector.memset(warm[:], 0.0)
+        nc.scalar.activation(later[:, 0:(E + 1) * W:PAIR], warm[:], GELU)
+
+        windows = [keep.tile([P, T], F32, name="window0")]
+        nc.vector.memset(windows[0][:], 0.0)
 
         token_words = keep.tile([P, T], I32, name="token_words", tag="token_words", align_bytes=64)
         nc.sync.dma_start(token_words[:], x_words[0].rearrange("p t r -> p (t r)").bitcast(I32))
         nc.sync.dma_start(bias, b.rearrange("(h p) e -> p h e", p=P))
-        load_w(2, nc.sync)
-        nc.sync.dma_start(gates[:, 0:PAIR], gate[0:P, 0:PAIR])
-        load_w(3, nc.sync)
-        nc.sync.dma_start(gates[:, PAIR:SLOTS], gate[0:P, PAIR:SLOTS])
-        for e in (E, 4, 5, 6, 7):
-            load_w(e, nc.sync)
+        for g in range(PAIRS):
+            load_w(2 * g + 2, nc.sync)
+            nc.sync.dma_start(gates[:, g * PAIR:(g + 1) * PAIR], gate[0:P, g * PAIR:(g + 1) * PAIR])
+            if g < PAIRS - 1:
+                load_w(2 * g + 3, nc.sync)
 
         weights = {}
 
@@ -91,18 +89,17 @@ def tile_moe_shr_lin_gelu_kernel(tc, x_words, x_scales, w, b, gate, offs, out):
             for i, e in enumerate(experts):
                 weights[e] = codes[:, i * N:(i + 1) * N], scales[:, i * N:(i + 1) * N]
 
-        slot_words = []
-
-        def gather_words(g, tag):
-            sw = keep.tile([P, PAIR], U32, name=f"slot_words{g}", tag=tag, align_bytes=64)
-            nc.vector.tensor_copy(sw[:], token_words[:].bitcast(U32).indirect(offsets[:, g * PAIR // 16:(g + 1) * PAIR // 16]))
-            slot_words.append(sw)
+        def gather_words(j0, j1):
+            sw = keep.tile([P, j1 - j0], U32, name=f"slot_words{j0}", align_bytes=64)
+            nc.vector.tensor_copy(sw[:], token_words[:].bitcast(U32).indirect(offsets[:, j0 // 16:j1 // 16]))
+            return [sw[:, j - j0:j - j0 + PAIR] for j in range(j0, j1, PAIR)]
 
         slot_scales = keep.tile([P, SLOTS], U8, name="slot_scales", align_bytes=64)
         nc.vector.tensor_copy(slot_scales[:], token_scales[:].indirect(offsets[:]))
         quantize(0, 1)
-        for g in range(PAIRS):
-            gather_words(g, f"slot_words{g}")
+        windows.append(keep.tile([P, T], F32, name="window1", tag="first1"))
+        nc.scalar.copy(windows[1][:], windows[0][:])
+        slot_words = gather_words(0, PAIR) + gather_words(PAIR, SLOTS)
 
         def routed(g, h, y):
             acc = routed_ps.tile([P, PAIR], F32, name="acc_routed")
@@ -143,21 +140,17 @@ def tile_moe_shr_lin_gelu_kernel(tc, x_words, x_scales, w, b, gate, offs, out):
             routed(g, 0, y0[:])
             quantize(2 * g + 2, 2 * g + 3)
             routed(g, 1, raw[2 * g + 3][:, 0:PAIR])
-            if g == 0:
-                quantize(E)
-        y_last = keep.tile([P, PAIR], F32, name="y_last")
-        routed(PAIRS - 1, 0, y_last[:])
+        quantize(E)
+        routed(PAIRS - 1, 0, raw[E][:, 0:PAIR])
 
-        ys_own = [keep.tile([P, CHUNK], F32, name=f"ys{i}") for i in range(CHUNKS - 2)]
-        ys_first = [raw[E - 2][:, 0:CHUNK], raw[E - 2][:, CHUNK:2 * CHUNK]] + [t[:] for t in ys_own]
-        ys_second = keep.tile([P, T], F32, name="ys_second")
+        ys = [keep.tile([P, T], F32, name=f"ys{h}") for h in range(HALVES)]
         for c in range(CHUNKS):
-            shared(0, c, ys_first[c])
+            shared(0, c, ys[0][:, c * CHUNK:(c + 1) * CHUNK])
+        for t0 in range(0, T, T // 2):
+            finish(0, t0, t0 + T // 2, ys[0][:, t0:t0 + T // 2])
+        routed(PAIRS - 1, 1, ys[0][:, 0:PAIR])
         for c in range(CHUNKS):
-            finish(0, c * CHUNK, (c + 1) * CHUNK, ys_first[c])
-        for c in range(CHUNKS):
-            shared(1, c, ys_second[:, c * CHUNK:(c + 1) * CHUNK])
-        routed(PAIRS - 1, 1, ys_first[2][:, 0:PAIR])
+            shared(1, c, ys[1][:, c * CHUNK:(c + 1) * CHUNK])
         cuts = [0, 256, 768, 1280, 1792, T]
         for t0, t1 in zip(cuts, cuts[1:]):
-            finish(1, t0, t1, ys_second[:, t0:t1])
+            finish(1, t0, t1, ys[1][:, t0:t1])

@@ -1,6 +1,7 @@
 from contextlib import ExitStack
 
 import concourse.mybir as mybir
+from concourse.masks import make_identity
 
 K, T, E, C, N = 512, 2048, 8, 128, 256
 SLOTS = E * C
@@ -32,8 +33,9 @@ def tile_moe_shr_lin_gelu_kernel(tc, x_words, x_scales, w, b, gate, offs, out):
     with ExitStack() as ctx:
         lists = ctx.enter_context(tc.tile_pool(name="lists", bufs=1))
         keep = ctx.enter_context(tc.tile_pool(name="keep", bufs=1))
-        routed_ps = ctx.enter_context(tc.psum_pool(name="routed_ps", bufs=4))
-        shared_ps = ctx.enter_context(tc.psum_pool(name="shared_ps", bufs=2))
+        psum = ctx.enter_context(tc.psum_pool(name="psum", bufs=1))
+
+        back_ps = ctx.enter_context(tc.psum_pool(name="back_ps", bufs=2))
 
         offsets = lists.tile([P, SLOTS // 16], U16, name="offsets")
         nc.sync.dma_start(offsets[:], offs)
@@ -60,24 +62,33 @@ def tile_moe_shr_lin_gelu_kernel(tc, x_words, x_scales, w, b, gate, offs, out):
         nc.vector.memset(warm[:], 0.0)
         nc.scalar.activation(later[:, 0:(E + 1) * W:PAIR], warm[:], GELU)
 
+        identity = keep.tile([P, P], F32, name="identity")
+        nc.vector.memset(identity[:], 0.0)
+        make_identity(nc, identity[:], nomemset=True)
+
         windows = [keep.tile([P, T], F32, name="window0")]
         nc.vector.memset(windows[0][:], 0.0)
 
         token_words = keep.tile([P, T], I32, name="token_words", tag="token_words", align_bytes=64)
         nc.sync.dma_start(token_words[:], x_words[0].rearrange("p t r -> p (t r)").bitcast(I32))
         nc.sync.dma_start(bias, b.rearrange("(h p) e -> p h e", p=P))
-        for g in range(PAIRS):
-            load_w(2 * g + 2, nc.sync)
+        def load_gate(g):
             nc.sync.dma_start(gates[:, g * PAIR:(g + 1) * PAIR], gate[0:P, g * PAIR:(g + 1) * PAIR])
-            if g < PAIRS - 1:
-                load_w(2 * g + 3, nc.sync)
+
+        for g in range(PAIRS - 1):
+            if g == 1:
+                load_w(E, nc.sync)
+            load_w(2 * g + 2, nc.sync)
+            load_gate(g)
+            load_w(2 * g + 3, nc.sync)
+        load_gate(PAIRS - 1)
 
         weights = {}
 
         def quantize(*experts):
             n = len(experts)
             e0 = experts[0]
-            grouped = keep.tile([P, n * W], BF16, name=f"grouped{e0}", align_bytes=64)
+            grouped = keep.tile([P, n * W], BF16, name=f"grouped{e0}", tag=f"grouped{e0}", align_bytes=64)
             for i, e in enumerate(experts):
                 nc.scalar.copy(
                     grouped[:, i * W:(i + 1) * W].rearrange("p (c i j) -> p c j i", i=4, j=PACK),
@@ -101,8 +112,8 @@ def tile_moe_shr_lin_gelu_kernel(tc, x_words, x_scales, w, b, gate, offs, out):
         nc.scalar.copy(windows[1][:], windows[0][:])
         slot_words = gather_words(0, PAIR) + gather_words(PAIR, SLOTS)
 
-        def routed(g, h, y):
-            acc = routed_ps.tile([P, PAIR], F32, name="acc_routed")
+        def routed(g, h, y, bank):
+            acc = psum.tile([P, PAIR], F32, name="acc_routed", tag=bank)
             cols = slice(h * P, (h + 1) * P)
             for i in range(2):
                 codes, scales = weights[2 * g + i]
@@ -118,9 +129,9 @@ def tile_moe_shr_lin_gelu_kernel(tc, x_words, x_scales, w, b, gate, offs, out):
                 nc.scalar.activation(y[:, i * C:(i + 1) * C], acc[:, i * C:(i + 1) * C], GELU, bias=bias[:, h, e:e + 1])
             nc.vector.tensor_tensor(windows[h][:].indirect(offsets[:, g * PAIR // 16:(g + 1) * PAIR // 16]), y, gates[:, g * PAIR:(g + 1) * PAIR], MULT)
 
-        def shared(h, c, ys):
+        def shared(h, c, ys, bank):
             codes, scales = weights[E]
-            acc = shared_ps.tile([P, CHUNK], F32, name="acc_shared")
+            acc = psum.tile([P, CHUNK], F32, name="acc_shared", tag=bank)
             cols = slice(h * P, (h + 1) * P)
             toks = slice(c * CHUNK, (c + 1) * CHUNK)
             nc.tensor.matmul_mx(
@@ -135,22 +146,58 @@ def tile_moe_shr_lin_gelu_kernel(tc, x_words, x_scales, w, b, gate, offs, out):
             nc.vector.tensor_tensor(total[:], windows[h][:, t0:t1], ys, ADD)
             nc.sync.dma_start(out[h * P:(h + 1) * P, t0:t1], total[:])
 
-        for g in range(PAIRS - 1):
-            y0 = keep.tile([P, PAIR], F32, name=f"y{g}")
-            routed(g, 0, y0[:])
-            quantize(2 * g + 2, 2 * g + 3)
-            routed(g, 1, raw[2 * g + 3][:, 0:PAIR])
-        quantize(E)
-        routed(PAIRS - 1, 0, raw[E][:, 0:PAIR])
+        def turn_and_add(c, ys, bank):
+            turned = psum.tile([P, CHUNK], F32, name="turned", tag=bank)
+            blocks = CHUNK // P
+            for s, source in enumerate((ys, windows[0][:, c * CHUNK:(c + 1) * CHUNK])):
+                for i in range(blocks):
+                    nc.tensor.matmul(
+                        turned[:, i * P:(i + 1) * P], lhsT=source[:, i * P:(i + 1) * P], rhs=identity[:], is_transpose=True,
+                        start=(s == 0 and i == 0), stop=(s == 1 and i == blocks - 1),
+                    )
+            sums = keep.tile([P, CHUNK], F32, name=f"sums{c}")
+            nc.scalar.copy(sums[:], turned[:])
+            return sums
 
-        ys = [keep.tile([P, T], F32, name=f"ys{h}") for h in range(HALVES)]
-        for c in range(CHUNKS):
-            shared(0, c, ys[0][:, c * CHUNK:(c + 1) * CHUNK])
-        for t0 in range(0, T, T // 2):
-            finish(0, t0, t0 + T // 2, ys[0][:, t0:t0 + T // 2])
-        routed(PAIRS - 1, 1, ys[0][:, 0:PAIR])
-        for c in range(CHUNKS):
-            shared(1, c, ys[1][:, c * CHUNK:(c + 1) * CHUNK])
+        def turn_back(c, sums):
+            back = back_ps.tile([P, CHUNK], F32, name="back")
+            for i in range(CHUNK // P):
+                nc.tensor.transpose(back[:, i * P:(i + 1) * P], sums[:, i * P:(i + 1) * P], identity[:])
+            total = keep.tile([P, CHUNK], F32, name=f"turned_total{c}")
+            nc.scalar.copy(total[:], back[:])
+            nc.scalar.dma_start(out[0:P, c * CHUNK:(c + 1) * CHUNK], total[:])
+
+        y_first = keep.tile([P, PAIR], F32, name="y_first")
+        routed(0, 0, y_first[:], "a")
+        quantize(2, 3)
+        routed(0, 1, raw[3][:, 0:PAIR], "b")
+        quantize(E)
+        quantize(4, 5)
+        routed(1, 0, raw[4][:, 0:PAIR], "a")
+        routed(1, 1, raw[5][:, 0:PAIR], "b")
+        quantize(6, 7)
+        routed(2, 0, raw[7][:, 0:PAIR], "a")
+
+        late = keep.tile([P, W], F32, name="late", tag="grouped6", align_bytes=64)
+        ys0_own = keep.tile([P, 2 * CHUNK], F32, name="ys0_own")
+        ys0 = [raw[7][:, PAIR:PAIR + CHUNK], ys0_own[:, 0:CHUNK], late[:, 0:CHUNK], ys0_own[:, CHUNK:2 * CHUNK]]
+        ys1 = keep.tile([P, T], F32, name="ys1")
+        y_last = keep.tile([P, PAIR], F32, name="y_last")
+        for c, bank in enumerate("dae"):
+            shared(0, c, ys0[c], bank)
+        routed(3, 0, y_last[:], "b")
+        for c in range(2):
+            finish(0, c * CHUNK, (c + 1) * CHUNK, ys0[c])
+        routed(2, 1, late[:, CHUNK:CHUNK + PAIR], "c")
+        routed(3, 1, late[:, CHUNK + PAIR:W], "b")
+        shared(0, 3, ys0[3], "d")
+        for c, bank in enumerate("ae"):
+            shared(1, c, ys1[:, c * CHUNK:(c + 1) * CHUNK], bank)
+        sums = [turn_and_add(c, ys0[c], bank) for c, bank in ((2, "d"), (3, "a"))]
+        shared(1, 2, ys1[:, 2 * CHUNK:3 * CHUNK], "e")
+        turn_back(2, sums[0])
+        shared(1, 3, ys1[:, 3 * CHUNK:4 * CHUNK], "d")
+        turn_back(3, sums[1])
         cuts = [0, 256, 768, 1280, 1792, T]
         for t0, t1 in zip(cuts, cuts[1:]):
-            finish(1, t0, t1, ys[1][:, t0:t1])
+            finish(1, t0, t1, ys1[:, t0:t1])

@@ -41,36 +41,36 @@ def tile_moe_shr_lin_gelu_kernel(tc, x_words, x_scales, w, b, gate, offs, out):
         nc.sync.dma_start(offsets[:], offs)
 
         W = PACK * N
-        first = [keep.tile([P, W], F32, name=f"first{e}", tag=f"first{e}") for e in range(2)]
-        later = keep.tile([P, (E + 1) * W], F32, name="later")
-        raw = [t[:] for t in first] + [later[:, (e - 2) * W:(e - 1) * W] for e in range(2, E + 1)]
-        gates = later[:, (E - 1) * W:E * W]
-        bias = later[:, E * W:E * W + HALVES * (E + 1)].rearrange("p (h e) -> p h e", h=HALVES)
-
-        def load_w(e, queue):
-            queue.dma_start(raw[e], w[e].rearrange("(p j) n -> p (j n)", j=PACK))
-
-        load_w(0, nc.scalar)
-        load_w(1, nc.scalar)
+        token_words = keep.tile([P, T], I32, name="token_words", align_bytes=64)
+        nc.sync.dma_start(token_words[:], x_words[0].rearrange("p t r -> p (t r)").bitcast(I32))
 
         token_scales = keep.tile([P, T], U8, name="token_scales", align_bytes=64)
         nc.vector.memset(token_scales[:].bitcast(I32), 0)
         for r in range(4):
             nc.sync.dma_start(token_scales[r:P:32, :].bitcast(I32), x_scales[0, r:16:4, :].bitcast(I32))
 
-        warm = keep.tile([P, (E + 1) * PACK], F32, name="warm", tag="token_words", align_bytes=64)
-        nc.vector.memset(warm[:], 0.0)
-        nc.scalar.activation(later[:, 0:(E + 1) * W:PAIR], warm[:], GELU)
+        windows = [keep.tile([P, T], F32, name=f"window{h}") for h in range(HALVES)]
+        zeros = keep.tile([P, 8], F32, name="zeros", tag="later")
+        nc.vector.memset(zeros[:], 0.0)
+        nc.scalar.activation(windows[0][:, 0:8], zeros[:], GELU)
 
         identity = keep.tile([P, P], F32, name="identity")
         nc.vector.memset(identity[:], 0.0)
         make_identity(nc, identity[:], nomemset=True)
 
-        windows = [keep.tile([P, T], F32, name="window0")]
-        nc.vector.memset(windows[0][:], 0.0)
+        nc.vector.memset(windows[0][:, 8:T], 0.0)
+        nc.scalar.copy(windows[1][:], windows[0][:])
 
-        token_words = keep.tile([P, T], I32, name="token_words", tag="token_words", align_bytes=64)
-        nc.sync.dma_start(token_words[:], x_words[0].rearrange("p t r -> p (t r)").bitcast(I32))
+        later = keep.tile([P, (E + 3) * W], F32, name="later", tag="later")
+        raw = [later[:, e * W:(e + 1) * W] for e in range(E + 1)]
+        gates = later[:, (E + 1) * W:(E + 2) * W]
+        bias = later[:, (E + 2) * W:(E + 2) * W + HALVES * (E + 1)].rearrange("p (h e) -> p h e", h=HALVES)
+
+        def load_w(e, queue):
+            queue.dma_start(raw[e], w[e].rearrange("(p j) n -> p (j n)", j=PACK))
+
+        load_w(0, nc.sync)
+        load_w(1, nc.sync)
         nc.sync.dma_start(bias, b.rearrange("(h p) e -> p h e", p=P))
         def load_gate(g):
             nc.sync.dma_start(gates[:, g * PAIR:(g + 1) * PAIR], gate[0:P, g * PAIR:(g + 1) * PAIR])
@@ -100,17 +100,17 @@ def tile_moe_shr_lin_gelu_kernel(tc, x_words, x_scales, w, b, gate, offs, out):
             for i, e in enumerate(experts):
                 weights[e] = codes[:, i * N:(i + 1) * N], scales[:, i * N:(i + 1) * N]
 
-        def gather_words(j0, j1):
-            sw = keep.tile([P, j1 - j0], U32, name=f"slot_words{j0}", align_bytes=64)
+        def gather_words(j0, j1, tag):
+            sw = keep.tile([P, j1 - j0], U32, name=f"slot_words{j0}", tag=tag, align_bytes=64)
             nc.vector.tensor_copy(sw[:], token_words[:].bitcast(U32).indirect(offsets[:, j0 // 16:j1 // 16]))
             return [sw[:, j - j0:j - j0 + PAIR] for j in range(j0, j1, PAIR)]
 
+        slot_words = gather_words(0, SLOTS // 2, "slot_words")
         slot_scales = keep.tile([P, SLOTS], U8, name="slot_scales", align_bytes=64)
         nc.vector.tensor_copy(slot_scales[:], token_scales[:].indirect(offsets[:]))
-        quantize(0, 1)
-        windows.append(keep.tile([P, T], F32, name="window1", tag="first1"))
-        nc.scalar.copy(windows[1][:], windows[0][:])
-        slot_words = gather_words(0, PAIR) + gather_words(PAIR, SLOTS)
+        quantize(0)
+        quantize(1)
+        slot_words = slot_words + gather_words(SLOTS // 2, SLOTS, "grouped1")
 
         def routed(g, h, y, bank):
             acc = psum.tile([P, PAIR], F32, name="acc_routed", tag=bank)

from contextlib import ExitStack

import concourse.mybir as mybir
from concourse.masks import make_identity

K, T, E, C, N = 512, 2048, 8, 128, 256
SLOTS = E * C
FLOPS = 2 * K * N * (T + SLOTS)
BYTES = K * T + 16 * T + (E + 1) * K * N * 4 + N * (E + 1) * 4 + SLOTS * 4 + 128 * (SLOTS // 16) * 2 + N * T * 4

F32 = mybir.dt.float32
BF16 = mybir.dt.bfloat16
I32 = mybir.dt.int32
U32 = mybir.dt.uint32
U16 = mybir.dt.uint16
U8 = mybir.dt.uint8
FP8X4 = mybir.dt.float8_e4m3fn_x4
GELU = mybir.ActivationFunctionType.Gelu_apprx_tanh
MULT = mybir.AluOpType.mult
ADD = mybir.AluOpType.add

P = 128
PACK = 4
HALVES = N // P
PAIR = 2 * C
PAIRS = E // 2
CHUNK = 512
CHUNKS = T // CHUNK


def tile_moe_shr_lin_gelu_kernel(tc, x_words, x_scales, w, b, gate, offs, out):
    nc = tc.nc
    with ExitStack() as ctx:
        lists = ctx.enter_context(tc.tile_pool(name="lists", bufs=1))
        keep = ctx.enter_context(tc.tile_pool(name="keep", bufs=1))
        psum = ctx.enter_context(tc.psum_pool(name="psum", bufs=1))

        back_ps = ctx.enter_context(tc.psum_pool(name="back_ps", bufs=2))

        offsets = lists.tile([P, SLOTS // 16], U16, name="offsets")
        nc.sync.dma_start(offsets[:], offs)

        W = PACK * N
        token_words = keep.tile([P, T], I32, name="token_words", align_bytes=64)
        nc.sync.dma_start(token_words[:], x_words[0].rearrange("p t r -> p (t r)").bitcast(I32))

        token_scales = keep.tile([P, T], U8, name="token_scales", align_bytes=64)
        nc.vector.memset(token_scales[:].bitcast(I32), 0)
        for r in range(4):
            nc.sync.dma_start(token_scales[r:P:32, :].bitcast(I32), x_scales[0, r:16:4, :].bitcast(I32))

        windows = [keep.tile([P, T], F32, name=f"window{h}") for h in range(HALVES)]
        zeros = keep.tile([P, 8], F32, name="zeros", tag="later")
        nc.vector.memset(zeros[:], 0.0)
        nc.scalar.activation(windows[0][:, 0:8], zeros[:], GELU)

        identity = keep.tile([P, P], F32, name="identity")
        nc.vector.memset(identity[:], 0.0)
        make_identity(nc, identity[:], nomemset=True)

        nc.vector.memset(windows[0][:, 8:T], 0.0)
        nc.scalar.copy(windows[1][:], windows[0][:])

        later = keep.tile([P, (E + 3) * W], F32, name="later", tag="later")
        raw = [later[:, e * W:(e + 1) * W] for e in range(E + 1)]
        gates = later[:, (E + 1) * W:(E + 2) * W]
        bias = later[:, (E + 2) * W:(E + 2) * W + HALVES * (E + 1)].rearrange("p (h e) -> p h e", h=HALVES)

        def load_w(e, queue):
            queue.dma_start(raw[e], w[e].rearrange("(p j) n -> p (j n)", j=PACK))

        load_w(0, nc.sync)
        load_w(1, nc.sync)
        nc.sync.dma_start(bias, b.rearrange("(h p) e -> p h e", p=P))
        def load_gate(g):
            nc.sync.dma_start(gates[:, g * PAIR:(g + 1) * PAIR], gate[0:P, g * PAIR:(g + 1) * PAIR])

        for g in range(PAIRS - 1):
            if g == 1:
                load_w(E, nc.sync)
            load_w(2 * g + 2, nc.sync)
            load_gate(g)
            load_w(2 * g + 3, nc.sync)
        load_gate(PAIRS - 1)

        weights = {}

        def quantize(*experts):
            n = len(experts)
            e0 = experts[0]
            grouped = keep.tile([P, n * W], BF16, name=f"grouped{e0}", tag=f"grouped{e0}", align_bytes=64)
            for i, e in enumerate(experts):
                nc.scalar.copy(
                    grouped[:, i * W:(i + 1) * W].rearrange("p (c i j) -> p c j i", i=4, j=PACK),
                    raw[e].rearrange("p (j c i) -> p c j i", i=4, j=PACK),
                )
            codes = keep.tile([P, n * N], U32, name=f"codes{e0}", align_bytes=64)
            scales = keep.tile([P, n * N], U8, name=f"scales{e0}", align_bytes=64)
            nc.vector.quantize_mx(out=codes[:].bitcast(FP8X4), scales=scales[:], in_=grouped[:])
            for i, e in enumerate(experts):
                weights[e] = codes[:, i * N:(i + 1) * N], scales[:, i * N:(i + 1) * N]

        def gather_words(j0, j1, tag):
            sw = keep.tile([P, j1 - j0], U32, name=f"slot_words{j0}", tag=tag, align_bytes=64)
            nc.vector.tensor_copy(sw[:], token_words[:].bitcast(U32).indirect(offsets[:, j0 // 16:j1 // 16]))
            return [sw[:, j - j0:j - j0 + PAIR] for j in range(j0, j1, PAIR)]

        slot_words = gather_words(0, SLOTS // 2, "slot_words")
        slot_scales = keep.tile([P, SLOTS], U8, name="slot_scales", align_bytes=64)
        nc.vector.tensor_copy(slot_scales[:], token_scales[:].indirect(offsets[:]))
        quantize(0)
        quantize(1)
        slot_words = slot_words + gather_words(SLOTS // 2, SLOTS, "grouped1")

        def routed(g, h, y, bank):
            acc = psum.tile([P, PAIR], F32, name="acc_routed", tag=bank)
            cols = slice(h * P, (h + 1) * P)
            for i in range(2):
                codes, scales = weights[2 * g + i]
                nc.tensor.matmul_mx(
                    out=acc[:, i * C:(i + 1) * C],
                    lhsT=codes[:, cols].bitcast(FP8X4), lhsT_scale=scales[:, cols],
                    rhs=slot_words[g][:, i * C:(i + 1) * C].bitcast(FP8X4),
                    rhs_scale=slot_scales[:, g * PAIR + i * C:g * PAIR + (i + 1) * C],
                    start=True, stop=True,
                )
            for i in range(2):
                e = 2 * g + i
                nc.scalar.activation(y[:, i * C:(i + 1) * C], acc[:, i * C:(i + 1) * C], GELU, bias=bias[:, h, e:e + 1])
            nc.vector.tensor_tensor(windows[h][:].indirect(offsets[:, g * PAIR // 16:(g + 1) * PAIR // 16]), y, gates[:, g * PAIR:(g + 1) * PAIR], MULT)

        def shared(h, c, ys, bank):
            codes, scales = weights[E]
            acc = psum.tile([P, CHUNK], F32, name="acc_shared", tag=bank)
            cols = slice(h * P, (h + 1) * P)
            toks = slice(c * CHUNK, (c + 1) * CHUNK)
            nc.tensor.matmul_mx(
                out=acc[:], lhsT=codes[:, cols].bitcast(FP8X4), lhsT_scale=scales[:, cols],
                rhs=token_words[:, toks].bitcast(FP8X4), rhs_scale=token_scales[:, toks],
                start=True, stop=True,
            )
            nc.scalar.activation(ys, acc[:], GELU, bias=bias[:, h, E:E + 1])

        def finish(h, t0, t1, ys):
            total = keep.tile([P, t1 - t0], F32, name=f"total{h}_{t0}")
            nc.vector.tensor_tensor(total[:], windows[h][:, t0:t1], ys, ADD)
            nc.sync.dma_start(out[h * P:(h + 1) * P, t0:t1], total[:])

        def turn_and_add(c, ys, bank):
            turned = psum.tile([P, CHUNK], F32, name="turned", tag=bank)
            blocks = CHUNK // P
            for s, source in enumerate((ys, windows[0][:, c * CHUNK:(c + 1) * CHUNK])):
                for i in range(blocks):
                    nc.tensor.matmul(
                        turned[:, i * P:(i + 1) * P], lhsT=source[:, i * P:(i + 1) * P], rhs=identity[:], is_transpose=True,
                        start=(s == 0 and i == 0), stop=(s == 1 and i == blocks - 1),
                    )
            sums = keep.tile([P, CHUNK], F32, name=f"sums{c}")
            nc.scalar.copy(sums[:], turned[:])
            return sums

        def turn_back(c, sums):
            back = back_ps.tile([P, CHUNK], F32, name="back")
            for i in range(CHUNK // P):
                nc.tensor.transpose(back[:, i * P:(i + 1) * P], sums[:, i * P:(i + 1) * P], identity[:])
            total = keep.tile([P, CHUNK], F32, name=f"turned_total{c}")
            nc.scalar.copy(total[:], back[:])
            nc.scalar.dma_start(out[0:P, c * CHUNK:(c + 1) * CHUNK], total[:])

        y_first = keep.tile([P, PAIR], F32, name="y_first")
        routed(0, 0, y_first[:], "a")
        quantize(2, 3)
        routed(0, 1, raw[3][:, 0:PAIR], "b")
        quantize(E)
        quantize(4, 5)
        routed(1, 0, raw[4][:, 0:PAIR], "a")
        routed(1, 1, raw[5][:, 0:PAIR], "b")
        quantize(6, 7)
        routed(2, 0, raw[7][:, 0:PAIR], "a")

        late = keep.tile([P, W], F32, name="late", tag="grouped6", align_bytes=64)
        ys0_own = keep.tile([P, 2 * CHUNK], F32, name="ys0_own")
        ys0 = [raw[7][:, PAIR:PAIR + CHUNK], ys0_own[:, 0:CHUNK], late[:, 0:CHUNK], ys0_own[:, CHUNK:2 * CHUNK]]
        ys1 = keep.tile([P, T], F32, name="ys1")
        y_last = keep.tile([P, PAIR], F32, name="y_last")
        for c, bank in enumerate("dae"):
            shared(0, c, ys0[c], bank)
        routed(3, 0, y_last[:], "b")
        for c in range(2):
            finish(0, c * CHUNK, (c + 1) * CHUNK, ys0[c])
        routed(2, 1, late[:, CHUNK:CHUNK + PAIR], "c")
        routed(3, 1, late[:, CHUNK + PAIR:W], "b")
        shared(0, 3, ys0[3], "d")
        for c, bank in enumerate("ae"):
            shared(1, c, ys1[:, c * CHUNK:(c + 1) * CHUNK], bank)
        sums = [turn_and_add(c, ys0[c], bank) for c, bank in ((2, "d"), (3, "a"))]
        shared(1, 2, ys1[:, 2 * CHUNK:3 * CHUNK], "e")
        turn_back(2, sums[0])
        shared(1, 3, ys1[:, 3 * CHUNK:4 * CHUNK], "d")
        turn_back(3, sums[1])
        cuts = [0, 256, 768, 1280, 1792, T]
        for t0, t1 in zip(cuts, cuts[1:]):
            finish(1, t0, t1, ys1[:, t0:t1])
